import numpy as np
import ml_dtypes


def mxq(x, axis, fmt="e4m3"):
    dtype, down = {"e4m3": (ml_dtypes.float8_e4m3fn, 7), "e5m2": (ml_dtypes.float8_e5m2, 14)}[fmt]
    v = np.moveaxis(np.asarray(x, np.float32).astype(ml_dtypes.bfloat16).astype(np.float64), axis, -1)
    blocks = v.reshape(v.shape[:-1] + (-1, 32))
    amax = np.abs(blocks).max(-1, keepdims=True)
    byte = np.maximum(np.where(amax > 0, np.frexp(amax)[1] - 1 + 127, 0) - down, 1)
    scale = np.exp2(byte - 127.0)
    codes = (blocks / scale).astype(np.float32).astype(dtype).astype(np.float64)
    return np.moveaxis((codes * scale).reshape(v.shape), -1, axis)


WIDE = False


def mx_kscale(k):
    if not WIDE:
        return np.ones(k)
    levels = np.array([10, -10, 5, -5, 0])
    if k % 512:
        return np.exp2(np.random.permutation(np.resize(levels, k // 32))).repeat(32)
    a = np.empty((k // 512, 16))
    for p in range(k // 512):
        a[p, :8] = np.random.permutation(np.resize(levels, 8))
        for g in range(8):
            far = levels[np.abs(levels - a[p, g]) >= 10]
            a[p, g + 8] = far[np.random.randint(len(far))]
    return np.exp2(a.ravel()).repeat(32)


def f64(x):
    return np.asarray(x).astype(np.float64)


def striped(idx):
    return np.tile(idx.reshape(-1, 16).T, (8, 1)).astype(np.uint16)


def unstriped(offs):
    return offs[:16].T.reshape(-1).astype(np.int64)


def striped8(idx):
    return np.concatenate([x.reshape(-1, 16).T for x in idx]).astype(np.uint16)


def runs(offs, k):
    lists = np.stack([offs[16 * r : 16 * r + 16].T.reshape(-1) for r in range(8)]).astype(np.int64)
    return lists[np.arange(k) % 512 // 64]


def pack_weight(w):
    k, n = w.shape
    w = f64(np.asarray(w, np.float32).astype(ml_dtypes.bfloat16)).reshape(k // 32, 32, n)
    amax = np.abs(w).max(1)
    byte = np.clip(np.where(amax > 0, np.frexp(amax)[1] - 1 + 127 - 7, 1), 1, 254)
    scaled = (w * np.exp2(127.0 - byte)[:, None, :]).reshape(k, n).astype(np.float32)
    words = np.ascontiguousarray(scaled.reshape(k // 512, 128, 4, n).transpose(0, 1, 3, 2)).astype(ml_dtypes.float8_e4m3fn).view(np.uint8)
    return words, np.ascontiguousarray(byte.astype(np.uint8).reshape(k // 512, 16, n))


def unpack_weight(words, scales):
    g, p, n, _ = words.shape
    vals = np.ascontiguousarray(words).view(ml_dtypes.float8_e4m3fn).astype(np.float64) * np.repeat(np.exp2(scales.astype(np.float64) - 127.0), 8, axis=1)[..., None]
    return vals.transpose(0, 1, 3, 2).reshape(g * 512, n)

def planes(y):
    n, m = y.shape
    v = y.astype(np.float32).astype(ml_dtypes.bfloat16).astype(np.float64).reshape(n // 32, 32, m)
    top = np.abs(v).max(1)
    byte = np.clip(np.where(top > 0, np.frexp(top)[1] - 1 + 127 - 7, 1), 1, 254)
    codes = (v * np.exp2(127.0 - byte)[:, None, :]).reshape(n, m).astype(np.float32).astype(ml_dtypes.float8_e4m3fn).view(np.uint8)
    words = codes.reshape(n // 512, 128, 4, m).transpose(0, 1, 3, 2)
    return np.ascontiguousarray(words), np.ascontiguousarray(byte.astype(np.uint8).reshape(n // 512, 16, m))


K, T, S, H, C = 512, 2048, 512, 512, 512


def setup_inputs():
    n = np.random.standard_normal
    s = mx_kscale(K)[:, None]
    packed_xT = pack_weight(n((K, T)) * s)
    packed_w1 = pack_weight(n((K, H)) / np.sqrt(K) / s)
    return {
        "x_words": packed_xT[0],
        "x_scales": packed_xT[1],
        "w1_words": packed_w1[0],
        "w1_scales": packed_w1[1],
        "gs": (np.random.uniform(0.5, 1.5, (K, 1)) / s).astype(np.float32),
        "wb": (n((K, S)) / np.sqrt(K) / s).astype(np.float32),
        "offs": striped(np.random.permutation(T)[:S]),
        "n1": striped8(np.stack([np.random.permutation(S) for _ in range(8)])),
        "n2": striped8(np.stack([np.random.permutation(S) for _ in range(8)])),
        "cand": striped(np.random.permutation(T)[:C]),
        "cb": striped(np.random.permutation(T)[:C]),
        "n3": striped8(np.stack([np.random.permutation(S) for _ in range(8)])),
        "n4": striped8(np.stack([np.random.permutation(S) for _ in range(8)])),
        "n5": striped8(np.stack([np.random.permutation(S) for _ in range(8)])),
    }


def reference(x_words, x_scales, w1_words, w1_scales, gs, wb, offs, n1, n2, cand, cb, n3, n4, n5):
    x_cand = unpack_weight(x_words, x_scales)[:, unstriped(cand)]
    xq = unpack_weight(x_words, x_scales)[:, unstriped(offs)]
    y = unpack_weight(w1_words, w1_scales).T @ xq
    z = f64(gs) * (0.75 * ((y - (y[np.arange(H)[:, None], runs(n1, H)])) * (y - (y[np.arange(H)[:, None], runs(n2, H)]))))
    a = 0.0625 * ((x_cand.T @ mxq(z, 0, "e4m3")))
    x_cb = unpack_weight(x_words, x_scales)[:, unstriped(cb)]
    b = x_cb.T @ mxq(f64(wb), 0, "e4m3")
    out_0 = np.maximum(np.minimum(a - (0.5 * (a[np.arange(C)[:, None], runs(n3, C)])), b[np.arange(C)[:, None], runs(n4, C)]), b[np.arange(C)[:, None], runs(n5, C)])
    return (out_0,) + planes(out_0)

@@ -1,0 +1,236 @@
+from contextlib import ExitStack
+
+import concourse.mybir as mybir
+
+K, T, S, H, C = 512, 2048, 512, 512, 512
+FLOPS = 3 * 2 * 512 * 512 * 512
+
+F32 = mybir.dt.float32
+BF16 = mybir.dt.bfloat16
+I32 = mybir.dt.int32
+U32 = mybir.dt.uint32
+U16 = mybir.dt.uint16
+U8 = mybir.dt.uint8
+FP8X4 = mybir.dt.float8_e4m3fn_x4
+ALU = mybir.AluOpType
+COPY = mybir.ActivationFunctionType.Copy
+
+P = 128
+PACK = 4
+HALF = S // 2
+LIST_COLS = S // 16
+VN2 = ((1, 0), (1, 1), (3, 0), (3, 1))
+VEA = (0,)
+SN3 = ((1, 0), (1, 1))
+BU = 2
+BL = 2
+
+
+def tile_picked_cdswclampbquad_none_po_kernel(
+    tc, x_words, x_scales, w1_words, w1_scales, gs, wb, offs, n1, n2, cand, cb, n3, n4, n5, out_0, out_1, out_2
+):
+    nc = tc.nc
+    with ExitStack() as ctx:
+        keep = ctx.enter_context(tc.tile_pool(name="keep", bufs=1))
+        psum = ctx.enter_context(tc.psum_pool(name="psum", bufs=1))
+
+        def sbuf(name, shape, dtype):
+            return keep.tile(shape, dtype, name=name, align_bytes=64)
+
+        def load_list(name, dram):
+            offsets = keep.tile([P, LIST_COLS], U16, name=name)
+            nc.sync.dma_start(offsets[:], dram)
+            return offsets
+
+        def load_scale_rows(plane, dram):
+            for q in range(4):
+                nc.sync.dma_start(plane[32 * q : 32 * q + 4, :].bitcast(I32), dram[0, 4 * q : 4 * q + 4, :].bitcast(I32))
+
+        def dealt(tile):
+            return tile[:].rearrange("p (t m) -> p m t", t=PACK)
+
+        def half_cols(h):
+            return slice(h * HALF, (h + 1) * HALF)
+
+        def half_list(offsets, h):
+            return offsets[:, h * LIST_COLS // 2 : (h + 1) * LIST_COLS // 2]
+
+        def gather(engine, dst, window, offsets, h):
+            src = window[:].indirect(half_list(offsets, h))
+            if engine == "vector":
+                nc.vector.tensor_copy(dst, src)
+            else:
+                nc.scalar.activation(dst, src, COPY)
+
+        def interleave(copy, grouped, rows, cols):
+            copy(
+                grouped[:, cols, :].rearrange("p (c i) t -> p c t i", i=4),
+                rows[:, :, cols].rearrange("p t (c i) -> p c t i", i=4),
+            )
+
+        def round_on_gpsimd(dst, src):
+            nc.gpsimd.tensor_scalar(dst, src, 1.0, 0.0, ALU.mult, ALU.add)
+
+        def quantize(codes, plane, grouped, cols):
+            nc.vector.quantize_mx(
+                out=codes[:, cols].bitcast(FP8X4),
+                scales=plane[:, cols],
+                in_=grouped[:, cols, :].rearrange("p c t -> p (c t)"),
+            )
+
+        def product(bank, lhs_codes, lhs_plane, t, rhs_codes, rhs_plane, cols):
+            m = slice(t * P, (t + 1) * P)
+            nc.tensor.matmul_mx(
+                out=bank[:, cols],
+                lhsT=lhs_codes[:, m].bitcast(FP8X4),
+                lhsT_scale=lhs_plane[:, m],
+                rhs=rhs_codes[:, cols].bitcast(FP8X4),
+                rhs_scale=rhs_plane[:, cols],
+                start=True,
+                stop=True,
+            )
+
+        whole = slice(0, S)
+
+        x_plane = sbuf("x_plane", [P, T], U8)
+        w1_plane_raw = sbuf("w1_plane_raw", [P, H], U8)
+        nc.vector.memset(x_plane[:].bitcast(I32), 0)
+        nc.gpsimd.memset(w1_plane_raw[:].bitcast(I32), 0)
+        x_codes = sbuf("x_codes", [P, T], I32)
+        w1_codes_raw = sbuf("w1_codes_raw", [P, H], I32)
+        offs_t = load_list("offs_t", offs)
+        gain = keep.tile([P, PACK], F32, name="gain", tag="staged_f32")
+        nc.sync.dma_start(gain[:], gs.rearrange("(p t) o -> p (t o)", t=PACK))
+        factor = sbuf("factor", [P, PACK], F32)
+        nc.gpsimd.tensor_scalar(factor[:], gain[:], 0.75, 0.0, ALU.mult, ALU.add)
+        n1_t = load_list("n1_t", n1)
+        n2_t = load_list("n2_t", n2)
+        nc.sync.dma_start(x_codes[:], x_words[0].rearrange("p n t -> p (n t)").bitcast(I32))
+        nc.sync.dma_start(w1_codes_raw[:], w1_words[0].rearrange("p n t -> p (n t)").bitcast(I32))
+        load_scale_rows(x_plane, x_scales)
+        load_scale_rows(w1_plane_raw, w1_scales)
+        n4_t = load_list("n4_t", n4)
+        n5_t = load_list("n5_t", n5)
+        cb_t = load_list("cb_t", cb)
+        cand_t = load_list("cand_t", cand)
+        wb_rows = keep.tile([P, PACK, S], F32, name="wb_rows", tag="staged_f32")
+        nc.sync.dma_start(wb_rows[:], wb.rearrange("(p t) n -> p t n", t=PACK))
+        n3_t = load_list("n3_t", n3)
+
+        xq_codes = sbuf("xq_codes", [P, S], U32)
+        xq_plane = sbuf("xq_plane", [P, S], U8)
+        cb_codes = sbuf("cb_codes", [P, C], U32)
+        cb_plane = sbuf("cb_plane", [P, C], U8)
+        cand_codes = sbuf("cand_codes", [P, C], U32)
+        cand_plane = sbuf("cand_plane", [P, C], U8)
+        w1_codes = sbuf("w1_codes", [P, H], U32)
+        w1_plane = sbuf("w1_plane", [P, H], U8)
+        x_window = x_codes[:].bitcast(U32)
+
+        nc.scalar.copy(
+            w1_codes[:].rearrange("p (t m) -> p t m", t=PACK),
+            w1_codes_raw[:].bitcast(U32).rearrange("p (m t) -> p t m", t=PACK),
+        )
+        nc.vector.tensor_copy(xq_plane[:], x_plane[:].indirect(offs_t[:]))
+        nc.vector.tensor_copy(xq_codes[:], x_window.indirect(offs_t[:]))
+        nc.gpsimd.tensor_copy(
+            w1_plane[:].rearrange("p (t m) -> p t m", t=PACK),
+            w1_plane_raw[:].rearrange("p (m t) -> p t m", t=PACK),
+        )
+        y_rows = [sbuf("y%d" % t, [P, S], F32) for t in range(PACK)]
+        y_banks = [psum.tile([P, S], F32, name="y_bank%d" % t, tag="first%d" % t) for t in range(PACK)]
+        for t in range(PACK):
+            product(y_banks[t], w1_codes, w1_plane, t, xq_codes, xq_plane, whole)
+        nc.vector.tensor_copy(dealt(cb_plane), x_plane[:].indirect(cb_t[:]))
+        nc.vector.tensor_copy(dealt(cb_codes), x_window.indirect(cb_t[:]))
+        nc.vector.tensor_copy(dealt(cand_plane), x_plane[:].indirect(cand_t[:]))
+        nc.vector.tensor_copy(dealt(cand_codes), x_window.indirect(cand_t[:]))
+
+        y_picked = [sbuf("y_picked%d" % t, [P, 2, S], F32) for t in range(PACK)]
+        y_diff = [sbuf("y_diff%d" % t, [P, 2, S], F32) for t in range(PACK)]
+        z_rows = sbuf("z_rows", [P, PACK, S], F32)
+        wb_grouped = sbuf("wb_grouped", [P, S, PACK], BF16)
+        wb_codes = sbuf("wb_codes", [P, S], U32)
+        wb_plane = sbuf("wb_plane", [P, S], U8)
+
+        for h in range(2):
+            interleave(round_on_gpsimd, wb_grouped, wb_rows, half_cols(h))
+        quantize(wb_codes, wb_plane, wb_grouped, whole)
+        b_banks = [psum.tile([P, S], F32, name="b_bank%d" % t, tag="second%d" % t) for t in range(PACK)]
+        for t in range(PACK):
+            product(b_banks[t], cb_codes, cb_plane, t, wb_codes, wb_plane, whole)
+
+        def z_tile(t):
+            nc.vector.scalar_tensor_tensor(
+                z_rows[:, t, :], y_diff[t][:, 0, :], factor[:, t : t + 1], y_diff[t][:, 1, :], ALU.mult, ALU.mult
+            )
+
+        for t in range(PACK):
+            nc.scalar.copy(y_rows[t][:], y_banks[t][:])
+            for h in range(2):
+                gather("scalar", y_picked[t][:, 0, half_cols(h)], y_rows[t], n1_t, h)
+            for h in range(2):
+                gather("vector" if (t, h) in VN2 else "scalar", y_picked[t][:, 1, half_cols(h)], y_rows[t], n2_t, h)
+            nc.vector.tensor_tensor(
+                y_diff[t][:], y_rows[t][:].unsqueeze(1).to_broadcast([P, 2, S]), y_picked[t][:], ALU.subtract
+            )
+            if t > 0:
+                z_tile(t - 1)
+        z_tile(PACK - 1)
+
+        z_grouped = sbuf("z_grouped", [P, S, PACK], BF16)
+        z_codes = sbuf("z_codes", [P, S], U32)
+        z_plane = sbuf("z_plane", [P, S], U8)
+        a_banks = [psum.tile([P, S], F32, name="a_bank%d" % t, tag="first%d" % t) for t in range(PACK)]
+        for h in range(2):
+            interleave(nc.vector.tensor_copy, z_grouped, z_rows, half_cols(h))
+        for h in range(2):
+            quantize(z_codes, z_plane, z_grouped, half_cols(h))
+        for t in range(PACK):
+            for h in range(2):
+                product(a_banks[t], cand_codes, cand_plane, t, z_codes, z_plane, half_cols(h))
+
+        b_rows = [sbuf("b%d" % t, [P, S], F32) for t in range(PACK)]
+        half_a = [sbuf("half_a%d" % t, [P, S], F32) for t in range(PACK)]
+        result = sbuf("result", [P, PACK, S], F32)
+        out_grouped = sbuf("out_grouped", [P, S, PACK], BF16)
+        out_codes = sbuf("out_codes", [P, S], U32)
+        out_plane = sbuf("out_plane", [P, S], U8)
+        out_rows = out_0.rearrange("(p t) n -> p t n", t=PACK)
+        out_words = out_1[0].rearrange("p n t -> p (n t)").bitcast(I32)
+        for t in range(PACK):
+            if t in VEA:
+                nc.vector.tensor_scalar(half_a[t][:], a_banks[t][:], 0.03125, None, ALU.mult)
+            else:
+                nc.scalar.activation(half_a[t][:], a_banks[t][:], COPY, scale=0.03125)
+            nc.scalar.copy(b_rows[t][:], b_banks[t][:])
+            upper = keep.tile([P, S], F32, name="upper", bufs=BU)
+            lower = keep.tile([P, S], F32, name="lower", bufs=BL)
+            a_picked = keep.tile([P, S], F32, name="a_picked", bufs=2)
+            score = keep.tile([P, S], F32, name="score", bufs=2)
+            capped = keep.tile([P, S], F32, name="capped", bufs=2)
+            for h in range(2):
+                gather("scalar" if (t, h) in SN3 else "vector", a_picked[:, half_cols(h)], half_a[t], n3_t, h)
+            for h in range(2):
+                gather("scalar", upper[:, half_cols(h)], b_rows[t], n4_t, h)
+            for h in range(2):
+                gather("scalar", lower[:, half_cols(h)], b_rows[t], n5_t, h)
+            nc.vector.scalar_tensor_tensor(score[:], half_a[t][:], 2.0, a_picked[:], ALU.mult, ALU.subtract)
+            nc.vector.tensor_tensor(capped[:], score[:], upper[:], ALU.min)
+            if t < PACK - 1:
+                nc.vector.tensor_tensor(result[:, t, :], capped[:], lower[:], ALU.max)
+                nc.sync.dma_start(out_rows[:, t, :], result[:, t, :])
+        last = PACK - 1
+        for h in range(2):
+            cols = half_cols(h)
+            nc.vector.tensor_tensor(result[:, last, cols], capped[:, cols], lower[:, cols], ALU.max)
+        nc.sync.dma_start(out_rows[:, last, :], result[:, last, :])
+        interleave(nc.scalar.copy, out_grouped, result, half_cols(0))
+        interleave(nc.vector.tensor_copy, out_grouped, result, half_cols(1))
+        for h in (1, 0):
+            cols = half_cols(h)
+            quantize(out_codes, out_plane, out_grouped, cols)
+        nc.sync.dma_start(out_words, out_codes[:].bitcast(I32))
+        for q in range(4):
+            queue = nc.sync if q % 2 == 0 else nc.scalar
+            queue.dma_start(out_2[0, 4 * q : 4 * q + 4, :].bitcast(I32), out_plane[32 * q : 32 * q + 4, :].bitcast(I32))

@@ -19,9 +19,15 @@ P = 128
 PACK = 4
 HALF = S // 2
 LIST_COLS = S // 16
-VN2 = ((1, 0), (1, 1), (3, 0), (3, 1))
+VN2 = ((1, 0), (1, 1), (2, 0), (2, 1))
 VEA = (0,)
-SN3 = ((1, 0), (1, 1))
+SN3 = ((1, 0), (1, 1), (2, 0), (2, 1))
+WS = ()
+FUSED = ()
+ZS = ()
+VB = ()
+DG = ()
+OS = 1
 BU = 2
 BL = 2
 
@@ -42,9 +48,9 @@ def tile_picked_cdswclampbquad_none_po_kernel(
             nc.sync.dma_start(offsets[:], dram)
             return offsets
 
-        def load_scale_rows(plane, dram):
-            for q in range(4):
-                nc.sync.dma_start(plane[32 * q : 32 * q + 4, :].bitcast(I32), dram[0, 4 * q : 4 * q + 4, :].bitcast(I32))
+        def load_scale_rows(plane, dram, queues):
+            for q, queue in enumerate(queues):
+                queue.dma_start(plane[32 * q : 32 * q + 4, :].bitcast(I32), dram[0, 4 * q : 4 * q + 4, :].bitcast(I32))
 
         def dealt(tile):
             return tile[:].rearrange("p (t m) -> p m t", t=PACK)
@@ -68,9 +74,6 @@ def tile_picked_cdswclampbquad_none_po_kernel(
                 rows[:, :, cols].rearrange("p t (c i) -> p c t i", i=4),
             )
 
-        def round_on_gpsimd(dst, src):
-            nc.gpsimd.tensor_scalar(dst, src, 1.0, 0.0, ALU.mult, ALU.add)
-
         def quantize(codes, plane, grouped, cols):
             nc.vector.quantize_mx(
                 out=codes[:, cols].bitcast(FP8X4),
@@ -92,6 +95,9 @@ def tile_picked_cdswclampbquad_none_po_kernel(
 
         whole = slice(0, S)
 
+        def pieces(t):
+            return [half_cols(0), half_cols(1)] if t == PACK - 1 else [whole]
+
         x_plane = sbuf("x_plane", [P, T], U8)
         w1_plane_raw = sbuf("w1_plane_raw", [P, H], U8)
         nc.vector.memset(x_plane[:].bitcast(I32), 0)
@@ -99,23 +105,23 @@ def tile_picked_cdswclampbquad_none_po_kernel(
         x_codes = sbuf("x_codes", [P, T], I32)
         w1_codes_raw = sbuf("w1_codes_raw", [P, H], I32)
         offs_t = load_list("offs_t", offs)
-        gain = keep.tile([P, PACK], F32, name="gain", tag="staged_f32")
-        nc.sync.dma_start(gain[:], gs.rearrange("(p t) o -> p (t o)", t=PACK))
-        factor = sbuf("factor", [P, PACK], F32)
-        nc.gpsimd.tensor_scalar(factor[:], gain[:], 0.75, 0.0, ALU.mult, ALU.add)
         n1_t = load_list("n1_t", n1)
-        n2_t = load_list("n2_t", n2)
         nc.sync.dma_start(x_codes[:], x_words[0].rearrange("p n t -> p (n t)").bitcast(I32))
         nc.sync.dma_start(w1_codes_raw[:], w1_words[0].rearrange("p n t -> p (n t)").bitcast(I32))
-        load_scale_rows(x_plane, x_scales)
-        load_scale_rows(w1_plane_raw, w1_scales)
+        load_scale_rows(x_plane, x_scales, [nc.sync] * 4)
+        load_scale_rows(w1_plane_raw, w1_scales, [nc.sync, nc.sync, nc.gpsimd, nc.gpsimd])
+        cb_t = load_list("cb_t", cb)
+        n2_t = load_list("n2_t", n2)
+        cand_t = load_list("cand_t", cand)
+        gain = sbuf("gain", [P, PACK], F32)
+        nc.sync.dma_start(gain[:], gs.rearrange("(p t) o -> p (t o)", t=PACK))
+        wb_rows = sbuf("wb_rows", [P, PACK, S], F32)
+        nc.sync.dma_start(wb_rows[:], wb.rearrange("(p t) n -> p t n", t=PACK))
         n4_t = load_list("n4_t", n4)
         n5_t = load_list("n5_t", n5)
-        cb_t = load_list("cb_t", cb)
-        cand_t = load_list("cand_t", cand)
-        wb_rows = keep.tile([P, PACK, S], F32, name="wb_rows", tag="staged_f32")
-        nc.sync.dma_start(wb_rows[:], wb.rearrange("(p t) n -> p t n", t=PACK))
         n3_t = load_list("n3_t", n3)
+        factor = sbuf("factor", [P, PACK], F32)
+        nc.gpsimd.tensor_scalar(factor[:], gain[:], 0.75, 0.0, ALU.mult, ALU.add)
 
         xq_codes = sbuf("xq_codes", [P, S], U32)
         xq_plane = sbuf("xq_plane", [P, S], U8)
@@ -133,7 +139,7 @@ def tile_picked_cdswclampbquad_none_po_kernel(
         )
         nc.vector.tensor_copy(xq_plane[:], x_plane[:].indirect(offs_t[:]))
         nc.vector.tensor_copy(xq_codes[:], x_window.indirect(offs_t[:]))
-        nc.gpsimd.tensor_copy(
+        nc.vector.tensor_copy(
             w1_plane[:].rearrange("p (t m) -> p t m", t=PACK),
             w1_plane_raw[:].rearrange("p (m t) -> p t m", t=PACK),
         )
@@ -154,26 +160,48 @@ def tile_picked_cdswclampbquad_none_po_kernel(
         wb_plane = sbuf("wb_plane", [P, S], U8)
 
         for h in range(2):
-            interleave(round_on_gpsimd, wb_grouped, wb_rows, half_cols(h))
+            interleave(nc.scalar.copy if h in WS else nc.vector.tensor_copy, wb_grouped, wb_rows, half_cols(h))
         quantize(wb_codes, wb_plane, wb_grouped, whole)
         b_banks = [psum.tile([P, S], F32, name="b_bank%d" % t, tag="second%d" % t) for t in range(PACK)]
         for t in range(PACK):
             product(b_banks[t], cb_codes, cb_plane, t, wb_codes, wb_plane, whole)
 
         def z_tile(t):
-            nc.vector.scalar_tensor_tensor(
-                z_rows[:, t, :], y_diff[t][:, 0, :], factor[:, t : t + 1], y_diff[t][:, 1, :], ALU.mult, ALU.mult
-            )
+            for cols in pieces(t):
+                nc.vector.scalar_tensor_tensor(
+                    z_rows[:, t, cols],
+                    y_diff[t][:, 0, cols],
+                    factor[:, t : t + 1],
+                    y_diff[t][:, 1, cols],
+                    ALU.mult,
+                    ALU.mult,
+                )
 
         for t in range(PACK):
             nc.scalar.copy(y_rows[t][:], y_banks[t][:])
-            for h in range(2):
-                gather("scalar", y_picked[t][:, 0, half_cols(h)], y_rows[t], n1_t, h)
-            for h in range(2):
-                gather("vector" if (t, h) in VN2 else "scalar", y_picked[t][:, 1, half_cols(h)], y_rows[t], n2_t, h)
-            nc.vector.tensor_tensor(
-                y_diff[t][:], y_rows[t][:].unsqueeze(1).to_broadcast([P, 2, S]), y_picked[t][:], ALU.subtract
-            )
+            if t in FUSED:
+                nc.scalar.copy(y_picked[t][:, 0, :], y_banks[t][:])
+                for side, offsets in enumerate((n1_t, n2_t)):
+                    for h in range(2):
+                        nc.vector.tensor_tensor(
+                            y_diff[t][:, side, half_cols(h)],
+                            y_rows[t][:].indirect(half_list(offsets, h)),
+                            y_picked[t][:, 0, half_cols(h)],
+                            ALU.subtract,
+                        )
+            else:
+                for h in range(2):
+                    gather("scalar", y_picked[t][:, 0, half_cols(h)], y_rows[t], n1_t, h)
+                for h in range(2):
+                    gather("vector" if (t, h) in VN2 else "scalar", y_picked[t][:, 1, half_cols(h)], y_rows[t], n2_t, h)
+                for cols in pieces(t):
+                    width = cols.stop - cols.start
+                    (nc.gpsimd if t in DG else nc.vector).tensor_tensor(
+                        y_diff[t][:, :, cols],
+                        y_rows[t][:, cols].unsqueeze(1).to_broadcast([P, 2, width]),
+                        y_picked[t][:, :, cols],
+                        ALU.subtract,
+                    )
             if t > 0:
                 z_tile(t - 1)
         z_tile(PACK - 1)
@@ -183,7 +211,7 @@ def tile_picked_cdswclampbquad_none_po_kernel(
         z_plane = sbuf("z_plane", [P, S], U8)
         a_banks = [psum.tile([P, S], F32, name="a_bank%d" % t, tag="first%d" % t) for t in range(PACK)]
         for h in range(2):
-            interleave(nc.vector.tensor_copy, z_grouped, z_rows, half_cols(h))
+            interleave(nc.scalar.copy if h in ZS else nc.vector.tensor_copy, z_grouped, z_rows, half_cols(h))
         for h in range(2):
             quantize(z_codes, z_plane, z_grouped, half_cols(h))
         for t in range(PACK):
@@ -212,25 +240,24 @@ def tile_picked_cdswclampbquad_none_po_kernel(
             for h in range(2):
                 gather("scalar" if (t, h) in SN3 else "vector", a_picked[:, half_cols(h)], half_a[t], n3_t, h)
             for h in range(2):
-                gather("scalar", upper[:, half_cols(h)], b_rows[t], n4_t, h)
+                gather("vector" if (4, t, h) in VB else "scalar", upper[:, half_cols(h)], b_rows[t], n4_t, h)
             for h in range(2):
-                gather("scalar", lower[:, half_cols(h)], b_rows[t], n5_t, h)
-            nc.vector.scalar_tensor_tensor(score[:], half_a[t][:], 2.0, a_picked[:], ALU.mult, ALU.subtract)
-            nc.vector.tensor_tensor(capped[:], score[:], upper[:], ALU.min)
-            if t < PACK - 1:
-                nc.vector.tensor_tensor(result[:, t, :], capped[:], lower[:], ALU.max)
-                nc.sync.dma_start(out_rows[:, t, :], result[:, t, :])
-        last = PACK - 1
-        for h in range(2):
-            cols = half_cols(h)
-            nc.vector.tensor_tensor(result[:, last, cols], capped[:, cols], lower[:, cols], ALU.max)
-        nc.sync.dma_start(out_rows[:, last, :], result[:, last, :])
-        interleave(nc.scalar.copy, out_grouped, result, half_cols(0))
+                gather("vector" if (5, t, h) in VB else "scalar", lower[:, half_cols(h)], b_rows[t], n5_t, h)
+            for cols in pieces(t):
+                nc.vector.scalar_tensor_tensor(
+                    score[:, cols], half_a[t][:, cols], 2.0, a_picked[:, cols], ALU.mult, ALU.subtract
+                )
+            for cols in pieces(t):
+                nc.vector.tensor_tensor(capped[:, cols], score[:, cols], upper[:, cols], ALU.min)
+            for cols in pieces(t):
+                nc.vector.tensor_tensor(result[:, t, cols], capped[:, cols], lower[:, cols], ALU.max)
+            nc.sync.dma_start(out_rows[:, t, :], result[:, t, :])
+        interleave(nc.scalar.copy if OS else nc.vector.tensor_copy, out_grouped, result, half_cols(0))
         interleave(nc.vector.tensor_copy, out_grouped, result, half_cols(1))
-        for h in (1, 0):
+        for h in ((1, 0) if OS else (0, 1)):
             cols = half_cols(h)
             quantize(out_codes, out_plane, out_grouped, cols)
-        nc.sync.dma_start(out_words, out_codes[:].bitcast(I32))
+            nc.sync.dma_start(out_words[:, cols], out_codes[:, cols].bitcast(I32))
         for q in range(4):
             queue = nc.sync if q % 2 == 0 else nc.scalar
             queue.dma_start(out_2[0, 4 * q : 4 * q + 4, :].bitcast(I32), out_plane[32 * q : 32 * q + 4, :].bitcast(I32))

@@ -2,7 +2,7 @@ from contextlib import ExitStack
 
 import concourse.mybir as mybir
 
-K, T, S, H, C = 512, 2048, 512, 512, 512
+T, S, H, C = 2048, 512, 512, 512
 FLOPS = 3 * 2 * 512 * 512 * 512
 
 F32 = mybir.dt.float32
@@ -17,19 +17,11 @@ COPY = mybir.ActivationFunctionType.Copy
 
 P = 128
 PACK = 4
+QUADRANTS = 4
 HALF = S // 2
-LIST_COLS = S // 16
-VN2 = ((1, 0), (1, 1), (2, 0), (2, 1))
-VEA = (0,)
-SN3 = ((1, 0), (1, 1), (2, 0), (2, 1))
-WS = ()
-FUSED = ()
-ZS = ()
-VB = ()
-DG = ()
-OS = 1
-BU = 2
-BL = 2
+VECTOR_CLEARS = 1408
+MIDDLE_TILES = (1, 2)
+BOUND_BUFS = 2
 
 
 def tile_picked_cdswclampbquad_none_po_kernel(
@@ -44,31 +36,37 @@ def tile_picked_cdswclampbquad_none_po_kernel(
             return keep.tile(shape, dtype, name=name, align_bytes=64)
 
         def load_list(name, dram):
-            offsets = keep.tile([P, LIST_COLS], U16, name=name)
+            offsets = keep.tile([P, S // 16], U16, name=name)
             nc.sync.dma_start(offsets[:], dram)
             return offsets
 
-        def load_scale_rows(plane, dram, queues):
-            for q, queue in enumerate(queues):
-                queue.dma_start(plane[32 * q : 32 * q + 4, :].bitcast(I32), dram[0, 4 * q : 4 * q + 4, :].bitcast(I32))
+        def plane_rows(plane, q):
+            return plane[32 * q : 32 * q + 4, :].bitcast(I32)
+
+        def dram_scale_rows(dram, q):
+            return dram[0, 4 * q : 4 * q + 4, :].bitcast(I32)
+
+        def dram_words(dram):
+            return dram[0].rearrange("p n t -> p (n t)").bitcast(I32)
+
+        def load_plane(plane, dram):
+            for q in range(QUADRANTS):
+                nc.sync.dma_start(plane_rows(plane, q), dram_scale_rows(dram, q))
 
         def dealt(tile):
             return tile[:].rearrange("p (t m) -> p m t", t=PACK)
 
-        def half_cols(h):
-            return slice(h * HALF, (h + 1) * HALF)
+        def deal(copy, dst, src):
+            copy(dst.rearrange("p (t m) -> p t m", t=PACK), src.rearrange("p (m t) -> p t m", t=PACK))
 
-        def half_list(offsets, h):
-            return offsets[:, h * LIST_COLS // 2 : (h + 1) * LIST_COLS // 2]
-
-        def gather(engine, dst, window, offsets, h):
-            src = window[:].indirect(half_list(offsets, h))
-            if engine == "vector":
+        def look_up(on_vector, dst, window, offsets):
+            src = window[:].indirect(offsets[:])
+            if on_vector:
                 nc.vector.tensor_copy(dst, src)
             else:
                 nc.scalar.activation(dst, src, COPY)
 
-        def interleave(copy, grouped, rows, cols):
+        def round_and_group(copy, grouped, rows, cols):
             copy(
                 grouped[:, cols, :].rearrange("p (c i) t -> p c t i", i=4),
                 rows[:, :, cols].rearrange("p t (c i) -> p c t i", i=4),
@@ -94,38 +92,40 @@ def tile_picked_cdswclampbquad_none_po_kernel(
             )
 
         whole = slice(0, S)
+        halves = [slice(0, HALF), slice(HALF, S)]
 
         def pieces(t):
-            return [half_cols(0), half_cols(1)] if t == PACK - 1 else [whole]
+            return halves if t == PACK - 1 else [whole]
 
         x_plane = sbuf("x_plane", [P, T], U8)
-        w1_plane_raw = sbuf("w1_plane_raw", [P, H], U8)
-        nc.vector.memset(x_plane[:].bitcast(I32), 0)
+        w1_plane_raw = keep.tile([P, H], U8, name="w1_plane_raw", tag="w1_plane_then_cb_codes", align_bytes=64)
+        nc.vector.memset(x_plane[:, :VECTOR_CLEARS].bitcast(I32), 0)
+        nc.gpsimd.memset(x_plane[:, VECTOR_CLEARS:].bitcast(I32), 0)
         nc.gpsimd.memset(w1_plane_raw[:].bitcast(I32), 0)
         x_codes = sbuf("x_codes", [P, T], I32)
         w1_codes_raw = sbuf("w1_codes_raw", [P, H], I32)
-        offs_t = load_list("offs_t", offs)
-        n1_t = load_list("n1_t", n1)
-        nc.sync.dma_start(x_codes[:], x_words[0].rearrange("p n t -> p (n t)").bitcast(I32))
-        nc.sync.dma_start(w1_codes_raw[:], w1_words[0].rearrange("p n t -> p (n t)").bitcast(I32))
-        load_scale_rows(x_plane, x_scales, [nc.sync] * 4)
-        load_scale_rows(w1_plane_raw, w1_scales, [nc.sync, nc.sync, nc.gpsimd, nc.gpsimd])
-        cb_t = load_list("cb_t", cb)
-        n2_t = load_list("n2_t", n2)
-        cand_t = load_list("cand_t", cand)
+        offs_list = load_list("offs_list", offs)
+        cb_list = load_list("cb_list", cb)
+        n1_list = load_list("n1_list", n1)
+        load_plane(x_plane, x_scales)
+        nc.sync.dma_start(x_codes[:], dram_words(x_words))
+        load_plane(w1_plane_raw, w1_scales)
+        nc.sync.dma_start(w1_codes_raw[:], dram_words(w1_words))
+        n2_list = load_list("n2_list", n2)
+        cand_list = load_list("cand_list", cand)
         gain = sbuf("gain", [P, PACK], F32)
         nc.sync.dma_start(gain[:], gs.rearrange("(p t) o -> p (t o)", t=PACK))
         wb_rows = sbuf("wb_rows", [P, PACK, S], F32)
         nc.sync.dma_start(wb_rows[:], wb.rearrange("(p t) n -> p t n", t=PACK))
-        n4_t = load_list("n4_t", n4)
-        n5_t = load_list("n5_t", n5)
-        n3_t = load_list("n3_t", n3)
-        factor = sbuf("factor", [P, PACK], F32)
-        nc.gpsimd.tensor_scalar(factor[:], gain[:], 0.75, 0.0, ALU.mult, ALU.add)
+        n4_list = load_list("n4_list", n4)
+        n5_list = load_list("n5_list", n5)
+        n3_list = load_list("n3_list", n3)
+        z_factor = sbuf("z_factor", [P, PACK], F32)
+        nc.gpsimd.tensor_scalar(z_factor[:], gain[:], 0.75, 0.0, ALU.mult, ALU.add)
 
         xq_codes = sbuf("xq_codes", [P, S], U32)
         xq_plane = sbuf("xq_plane", [P, S], U8)
-        cb_codes = sbuf("cb_codes", [P, C], U32)
+        cb_codes = keep.tile([P, C], U32, name="cb_codes", tag="w1_plane_then_cb_codes", align_bytes=64)
         cb_plane = sbuf("cb_plane", [P, C], U8)
         cand_codes = sbuf("cand_codes", [P, C], U32)
         cand_plane = sbuf("cand_plane", [P, C], U8)
@@ -133,131 +133,109 @@ def tile_picked_cdswclampbquad_none_po_kernel(
         w1_plane = sbuf("w1_plane", [P, H], U8)
         x_window = x_codes[:].bitcast(U32)
 
-        nc.scalar.copy(
-            w1_codes[:].rearrange("p (t m) -> p t m", t=PACK),
-            w1_codes_raw[:].bitcast(U32).rearrange("p (m t) -> p t m", t=PACK),
-        )
-        nc.vector.tensor_copy(xq_plane[:], x_plane[:].indirect(offs_t[:]))
-        nc.vector.tensor_copy(xq_codes[:], x_window.indirect(offs_t[:]))
-        nc.vector.tensor_copy(
-            w1_plane[:].rearrange("p (t m) -> p t m", t=PACK),
-            w1_plane_raw[:].rearrange("p (m t) -> p t m", t=PACK),
-        )
-        y_rows = [sbuf("y%d" % t, [P, S], F32) for t in range(PACK)]
-        y_banks = [psum.tile([P, S], F32, name="y_bank%d" % t, tag="first%d" % t) for t in range(PACK)]
+        deal(nc.scalar.copy, w1_codes[:], w1_codes_raw[:].bitcast(U32))
+        nc.vector.tensor_copy(xq_plane[:], x_plane[:].indirect(offs_list[:]))
+        nc.vector.tensor_copy(xq_codes[:], x_window.indirect(offs_list[:]))
+        deal(nc.vector.tensor_copy, w1_plane[:], w1_plane_raw[:])
+
+        ya_window = [sbuf("ya_window%d" % t, [P, 2 * S], F32) for t in range(PACK)]
+        b_window = [sbuf("b_window%d" % t, [P, 3 * S], F32) for t in range(PACK)]
+        for t in range(PACK):
+            nc.vector.memset(ya_window[t][:, S:].bitcast(I32), 0)
+        y_banks = [psum.tile([P, S], F32, name="y_bank%d" % t, tag="y_then_a%d" % t) for t in range(PACK)]
         for t in range(PACK):
             product(y_banks[t], w1_codes, w1_plane, t, xq_codes, xq_plane, whole)
-        nc.vector.tensor_copy(dealt(cb_plane), x_plane[:].indirect(cb_t[:]))
-        nc.vector.tensor_copy(dealt(cb_codes), x_window.indirect(cb_t[:]))
-        nc.vector.tensor_copy(dealt(cand_plane), x_plane[:].indirect(cand_t[:]))
-        nc.vector.tensor_copy(dealt(cand_codes), x_window.indirect(cand_t[:]))
+        nc.vector.tensor_copy(dealt(cb_plane), x_plane[:].indirect(cb_list[:]))
+        nc.vector.tensor_copy(dealt(cb_codes), x_window.indirect(cb_list[:]))
+        nc.vector.tensor_copy(dealt(cand_plane), x_plane[:].indirect(cand_list[:]))
+        nc.vector.tensor_copy(dealt(cand_codes), x_window.indirect(cand_list[:]))
 
-        y_picked = [sbuf("y_picked%d" % t, [P, 2, S], F32) for t in range(PACK)]
-        y_diff = [sbuf("y_diff%d" % t, [P, 2, S], F32) for t in range(PACK)]
-        z_rows = sbuf("z_rows", [P, PACK, S], F32)
         wb_grouped = sbuf("wb_grouped", [P, S, PACK], BF16)
         wb_codes = sbuf("wb_codes", [P, S], U32)
         wb_plane = sbuf("wb_plane", [P, S], U8)
-
-        for h in range(2):
-            interleave(nc.scalar.copy if h in WS else nc.vector.tensor_copy, wb_grouped, wb_rows, half_cols(h))
+        for cols in halves:
+            round_and_group(nc.vector.tensor_copy, wb_grouped, wb_rows, cols)
         quantize(wb_codes, wb_plane, wb_grouped, whole)
-        b_banks = [psum.tile([P, S], F32, name="b_bank%d" % t, tag="second%d" % t) for t in range(PACK)]
+        b_banks = [psum.tile([P, S], F32, name="b_bank%d" % t, tag="b%d" % t) for t in range(PACK)]
         for t in range(PACK):
             product(b_banks[t], cb_codes, cb_plane, t, wb_codes, wb_plane, whole)
 
-        def z_tile(t):
+        y_picked = [sbuf("y_picked%d" % t, [P, 2, S], F32) for t in range(PACK)]
+        y_diff = [b_window[t][:, S:].rearrange("p (side c) -> p side c", side=2) for t in range(PACK)]
+        z_rows = sbuf("z_rows", [P, PACK, S], F32)
+
+        def multiply_differences(t):
             for cols in pieces(t):
                 nc.vector.scalar_tensor_tensor(
                     z_rows[:, t, cols],
                     y_diff[t][:, 0, cols],
-                    factor[:, t : t + 1],
+                    z_factor[:, t : t + 1],
                     y_diff[t][:, 1, cols],
                     ALU.mult,
                     ALU.mult,
                 )
 
         for t in range(PACK):
-            nc.scalar.copy(y_rows[t][:], y_banks[t][:])
-            if t in FUSED:
-                nc.scalar.copy(y_picked[t][:, 0, :], y_banks[t][:])
-                for side, offsets in enumerate((n1_t, n2_t)):
-                    for h in range(2):
-                        nc.vector.tensor_tensor(
-                            y_diff[t][:, side, half_cols(h)],
-                            y_rows[t][:].indirect(half_list(offsets, h)),
-                            y_picked[t][:, 0, half_cols(h)],
-                            ALU.subtract,
-                        )
-            else:
-                for h in range(2):
-                    gather("scalar", y_picked[t][:, 0, half_cols(h)], y_rows[t], n1_t, h)
-                for h in range(2):
-                    gather("vector" if (t, h) in VN2 else "scalar", y_picked[t][:, 1, half_cols(h)], y_rows[t], n2_t, h)
-                for cols in pieces(t):
-                    width = cols.stop - cols.start
-                    (nc.gpsimd if t in DG else nc.vector).tensor_tensor(
-                        y_diff[t][:, :, cols],
-                        y_rows[t][:, cols].unsqueeze(1).to_broadcast([P, 2, width]),
-                        y_picked[t][:, :, cols],
-                        ALU.subtract,
-                    )
+            y_rows = ya_window[t][:, :S]
+            nc.scalar.copy(y_rows, y_banks[t][:])
+            look_up(False, y_picked[t][:, 0, :], ya_window[t], n1_list)
+            look_up(t in MIDDLE_TILES, y_picked[t][:, 1, :], ya_window[t], n2_list)
+            for cols in pieces(t):
+                nc.vector.tensor_tensor(
+                    y_diff[t][:, :, cols],
+                    y_rows[:, cols].unsqueeze(1).to_broadcast([P, 2, cols.stop - cols.start]),
+                    y_picked[t][:, :, cols],
+                    ALU.subtract,
+                )
             if t > 0:
-                z_tile(t - 1)
-        z_tile(PACK - 1)
+                multiply_differences(t - 1)
+        multiply_differences(PACK - 1)
 
         z_grouped = sbuf("z_grouped", [P, S, PACK], BF16)
         z_codes = sbuf("z_codes", [P, S], U32)
         z_plane = sbuf("z_plane", [P, S], U8)
-        a_banks = [psum.tile([P, S], F32, name="a_bank%d" % t, tag="first%d" % t) for t in range(PACK)]
-        for h in range(2):
-            interleave(nc.scalar.copy if h in ZS else nc.vector.tensor_copy, z_grouped, z_rows, half_cols(h))
-        for h in range(2):
-            quantize(z_codes, z_plane, z_grouped, half_cols(h))
+        a_banks = [psum.tile([P, S], F32, name="a_bank%d" % t, tag="y_then_a%d" % t) for t in range(PACK)]
+        for cols in halves:
+            round_and_group(nc.vector.tensor_copy, z_grouped, z_rows, cols)
+        for cols in halves:
+            quantize(z_codes, z_plane, z_grouped, cols)
         for t in range(PACK):
-            for h in range(2):
-                product(a_banks[t], cand_codes, cand_plane, t, z_codes, z_plane, half_cols(h))
+            for cols in halves:
+                product(a_banks[t], cand_codes, cand_plane, t, z_codes, z_plane, cols)
 
-        b_rows = [sbuf("b%d" % t, [P, S], F32) for t in range(PACK)]
-        half_a = [sbuf("half_a%d" % t, [P, S], F32) for t in range(PACK)]
         result = sbuf("result", [P, PACK, S], F32)
+        out_rows = out_0.rearrange("(p t) n -> p t n", t=PACK)
+        for t in range(PACK):
+            half_a = ya_window[t][:, :S]
+            if t == 0:
+                nc.vector.tensor_scalar(half_a, a_banks[t][:], 1.0 / 32, None, ALU.mult)
+            else:
+                nc.scalar.activation(half_a, a_banks[t][:], COPY, scale=1.0 / 32)
+            nc.scalar.copy(b_window[t][:, :S], b_banks[t][:])
+            upper = keep.tile([P, S], F32, name="upper", bufs=BOUND_BUFS)
+            lower = keep.tile([P, S], F32, name="lower", bufs=BOUND_BUFS)
+            half_a_picked = keep.tile([P, S], F32, name="half_a_picked", bufs=PACK)
+            score = keep.tile([P, S], F32, name="score", bufs=PACK)
+            capped = keep.tile([P, S], F32, name="capped", bufs=PACK)
+            look_up(t not in MIDDLE_TILES, half_a_picked[:], ya_window[t], n3_list)
+            look_up(False, upper[:], b_window[t], n4_list)
+            look_up(False, lower[:], b_window[t], n5_list)
+            for cols in pieces(t):
+                nc.vector.scalar_tensor_tensor(
+                    score[:, cols], half_a[:, cols], 2.0, half_a_picked[:, cols], ALU.mult, ALU.subtract
+                )
+                nc.vector.tensor_tensor(capped[:, cols], score[:, cols], upper[:, cols], ALU.min)
+                nc.vector.tensor_tensor(result[:, t, cols], capped[:, cols], lower[:, cols], ALU.max)
+            nc.sync.dma_start(out_rows[:, t, :], result[:, t, :])
+
         out_grouped = sbuf("out_grouped", [P, S, PACK], BF16)
         out_codes = sbuf("out_codes", [P, S], U32)
         out_plane = sbuf("out_plane", [P, S], U8)
-        out_rows = out_0.rearrange("(p t) n -> p t n", t=PACK)
-        out_words = out_1[0].rearrange("p n t -> p (n t)").bitcast(I32)
-        for t in range(PACK):
-            if t in VEA:
-                nc.vector.tensor_scalar(half_a[t][:], a_banks[t][:], 0.03125, None, ALU.mult)
-            else:
-                nc.scalar.activation(half_a[t][:], a_banks[t][:], COPY, scale=0.03125)
-            nc.scalar.copy(b_rows[t][:], b_banks[t][:])
-            upper = keep.tile([P, S], F32, name="upper", bufs=BU)
-            lower = keep.tile([P, S], F32, name="lower", bufs=BL)
-            a_picked = keep.tile([P, S], F32, name="a_picked", bufs=2)
-            score = keep.tile([P, S], F32, name="score", bufs=2)
-            capped = keep.tile([P, S], F32, name="capped", bufs=2)
-            for h in range(2):
-                gather("scalar" if (t, h) in SN3 else "vector", a_picked[:, half_cols(h)], half_a[t], n3_t, h)
-            for h in range(2):
-                gather("vector" if (4, t, h) in VB else "scalar", upper[:, half_cols(h)], b_rows[t], n4_t, h)
-            for h in range(2):
-                gather("vector" if (5, t, h) in VB else "scalar", lower[:, half_cols(h)], b_rows[t], n5_t, h)
-            for cols in pieces(t):
-                nc.vector.scalar_tensor_tensor(
-                    score[:, cols], half_a[t][:, cols], 2.0, a_picked[:, cols], ALU.mult, ALU.subtract
-                )
-            for cols in pieces(t):
-                nc.vector.tensor_tensor(capped[:, cols], score[:, cols], upper[:, cols], ALU.min)
-            for cols in pieces(t):
-                nc.vector.tensor_tensor(result[:, t, cols], capped[:, cols], lower[:, cols], ALU.max)
-            nc.sync.dma_start(out_rows[:, t, :], result[:, t, :])
-        interleave(nc.scalar.copy if OS else nc.vector.tensor_copy, out_grouped, result, half_cols(0))
-        interleave(nc.vector.tensor_copy, out_grouped, result, half_cols(1))
-        for h in ((1, 0) if OS else (0, 1)):
-            cols = half_cols(h)
+        round_and_group(nc.scalar.copy, out_grouped, result, halves[0])
+        round_and_group(nc.vector.tensor_copy, out_grouped, result, halves[1])
+        for cols in reversed(halves):
             quantize(out_codes, out_plane, out_grouped, cols)
-            nc.sync.dma_start(out_words[:, cols], out_codes[:, cols].bitcast(I32))
-        for q in range(4):
+            nc.sync.dma_start(dram_words(out_1)[:, cols], out_codes[:, cols].bitcast(I32))
+        for q in range(QUADRANTS):
             queue = nc.sync if q % 2 == 0 else nc.scalar
-            queue.dma_start(out_2[0, 4 * q : 4 * q + 4, :].bitcast(I32), out_plane[32 * q : 32 * q + 4, :].bitcast(I32))
+            queue.dma_start(dram_scale_rows(out_2, q), plane_rows(out_plane, q))

@@ -20,8 +20,8 @@ PACK = 4
 QUADRANTS = 4
 HALF = S // 2
 VECTOR_CLEARS = 1408
-MIDDLE_TILES = (1, 2)
-BOUND_BUFS = 2
+UPPER_BUFS = 2
+LOWER_BUFS = 3
 
 
 def tile_picked_cdswclampbquad_none_po_kernel(
@@ -57,7 +57,10 @@ def tile_picked_cdswclampbquad_none_po_kernel(
             return tile[:].rearrange("p (t m) -> p m t", t=PACK)
 
         def deal(copy, dst, src):
-            copy(dst.rearrange("p (t m) -> p t m", t=PACK), src.rearrange("p (m t) -> p t m", t=PACK))
+            src_by_tile = src.rearrange("p (c i t) -> p c t i", i=4, t=PACK)
+            dst_by_tile = dst.rearrange("p (t c i) -> p c t i", i=4, t=PACK)
+            for tiles in (slice(0, 1), slice(1, PACK)):
+                copy(dst_by_tile[:, :, tiles, :], src_by_tile[:, :, tiles, :])
 
         def look_up(on_vector, dst, window, offsets):
             src = window[:].indirect(offsets[:])
@@ -160,7 +163,6 @@ def tile_picked_cdswclampbquad_none_po_kernel(
         for t in range(PACK):
             product(b_banks[t], cb_codes, cb_plane, t, wb_codes, wb_plane, whole)
 
-        y_picked = [sbuf("y_picked%d" % t, [P, 2, S], F32) for t in range(PACK)]
         y_diff = [b_window[t][:, S:].rearrange("p (side c) -> p side c", side=2) for t in range(PACK)]
         z_rows = sbuf("z_rows", [P, PACK, S], F32)
 
@@ -178,15 +180,20 @@ def tile_picked_cdswclampbquad_none_po_kernel(
         for t in range(PACK):
             y_rows = ya_window[t][:, :S]
             nc.scalar.copy(y_rows, y_banks[t][:])
-            look_up(False, y_picked[t][:, 0, :], ya_window[t], n1_list)
-            look_up(t in MIDDLE_TILES, y_picked[t][:, 1, :], ya_window[t], n2_list)
-            for cols in pieces(t):
+            if t % 2 == 1:
+                y_picked = sbuf("y_picked%d" % t, [P, 2, S], F32)
+                for side, offsets in enumerate((n1_list, n2_list)):
+                    nc.scalar.activation(y_picked[:, side, :], ya_window[t][:].indirect(offsets[:]), COPY)
                 nc.vector.tensor_tensor(
-                    y_diff[t][:, :, cols],
-                    y_rows[:, cols].unsqueeze(1).to_broadcast([P, 2, cols.stop - cols.start]),
-                    y_picked[t][:, :, cols],
-                    ALU.subtract,
+                    y_diff[t], y_picked[:], y_rows.unsqueeze(1).to_broadcast([P, 2, S]), ALU.subtract
                 )
+            else:
+                y_copy = sbuf("y_copy%d" % t, [P, S], F32)
+                nc.scalar.copy(y_copy[:], y_banks[t][:])
+                for side, offsets in enumerate((n1_list, n2_list)):
+                    nc.vector.tensor_tensor(
+                        y_diff[t][:, side, :], ya_window[t][:].indirect(offsets[:]), y_copy[:], ALU.subtract
+                    )
             if t > 0:
                 multiply_differences(t - 1)
         multiply_differences(PACK - 1)
@@ -212,19 +219,17 @@ def tile_picked_cdswclampbquad_none_po_kernel(
             else:
                 nc.scalar.activation(half_a, a_banks[t][:], COPY, scale=1.0 / 32)
             nc.scalar.copy(b_window[t][:, :S], b_banks[t][:])
-            upper = keep.tile([P, S], F32, name="upper", bufs=BOUND_BUFS)
-            lower = keep.tile([P, S], F32, name="lower", bufs=BOUND_BUFS)
+            upper = keep.tile([P, S], F32, name="upper", bufs=UPPER_BUFS)
+            lower = keep.tile([P, S], F32, name="lower", bufs=LOWER_BUFS)
             half_a_picked = keep.tile([P, S], F32, name="half_a_picked", bufs=PACK)
             score = keep.tile([P, S], F32, name="score", bufs=PACK)
             capped = keep.tile([P, S], F32, name="capped", bufs=PACK)
-            look_up(t not in MIDDLE_TILES, half_a_picked[:], ya_window[t], n3_list)
+            look_up(t == 0, half_a_picked[:], ya_window[t], n3_list)
             look_up(False, upper[:], b_window[t], n4_list)
             look_up(False, lower[:], b_window[t], n5_list)
+            nc.vector.scalar_tensor_tensor(score[:], half_a, 2.0, half_a_picked[:], ALU.mult, ALU.subtract)
+            nc.vector.tensor_tensor(capped[:], score[:], upper[:], ALU.min)
             for cols in pieces(t):
-                nc.vector.scalar_tensor_tensor(
-                    score[:, cols], half_a[:, cols], 2.0, half_a_picked[:, cols], ALU.mult, ALU.subtract
-                )
-                nc.vector.tensor_tensor(capped[:, cols], score[:, cols], upper[:, cols], ALU.min)
                 nc.vector.tensor_tensor(result[:, t, cols], capped[:, cols], lower[:, cols], ALU.max)
             nc.sync.dma_start(out_rows[:, t, :], result[:, t, :])
 

from contextlib import ExitStack

import concourse.mybir as mybir

T, S, H, C = 2048, 512, 512, 512
FLOPS = 3 * 2 * 512 * 512 * 512

F32 = mybir.dt.float32
BF16 = mybir.dt.bfloat16
I32 = mybir.dt.int32
U32 = mybir.dt.uint32
U16 = mybir.dt.uint16
U8 = mybir.dt.uint8
FP8X4 = mybir.dt.float8_e4m3fn_x4
ALU = mybir.AluOpType
COPY = mybir.ActivationFunctionType.Copy

P = 128
PACK = 4
QUADRANTS = 4
HALF = S // 2
VECTOR_CLEARS = 1408
UPPER_BUFS = 2
LOWER_BUFS = 3


def tile_picked_cdswclampbquad_none_po_kernel(
    tc, x_words, x_scales, w1_words, w1_scales, gs, wb, offs, n1, n2, cand, cb, n3, n4, n5, out_0, out_1, out_2
):
    nc = tc.nc
    with ExitStack() as ctx:
        keep = ctx.enter_context(tc.tile_pool(name="keep", bufs=1))
        psum = ctx.enter_context(tc.psum_pool(name="psum", bufs=1))

        def sbuf(name, shape, dtype):
            return keep.tile(shape, dtype, name=name, align_bytes=64)

        def load_list(name, dram):
            offsets = keep.tile([P, S // 16], U16, name=name)
            nc.sync.dma_start(offsets[:], dram)
            return offsets

        def plane_rows(plane, q):
            return plane[32 * q : 32 * q + 4, :].bitcast(I32)

        def dram_scale_rows(dram, q):
            return dram[0, 4 * q : 4 * q + 4, :].bitcast(I32)

        def dram_words(dram):
            return dram[0].rearrange("p n t -> p (n t)").bitcast(I32)

        def load_plane(plane, dram):
            for q in range(QUADRANTS):
                nc.sync.dma_start(plane_rows(plane, q), dram_scale_rows(dram, q))

        def dealt(tile):
            return tile[:].rearrange("p (t m) -> p m t", t=PACK)

        def deal(copy, dst, src):
            src_by_tile = src.rearrange("p (c i t) -> p c t i", i=4, t=PACK)
            dst_by_tile = dst.rearrange("p (t c i) -> p c t i", i=4, t=PACK)
            for tiles in (slice(0, 1), slice(1, PACK)):
                copy(dst_by_tile[:, :, tiles, :], src_by_tile[:, :, tiles, :])

        def look_up(on_vector, dst, window, offsets):
            src = window[:].indirect(offsets[:])
            if on_vector:
                nc.vector.tensor_copy(dst, src)
            else:
                nc.scalar.activation(dst, src, COPY)

        def round_and_group(copy, grouped, rows, cols):
            copy(
                grouped[:, cols, :].rearrange("p (c i) t -> p c t i", i=4),
                rows[:, :, cols].rearrange("p t (c i) -> p c t i", i=4),
            )

        def quantize(codes, plane, grouped, cols):
            nc.vector.quantize_mx(
                out=codes[:, cols].bitcast(FP8X4),
                scales=plane[:, cols],
                in_=grouped[:, cols, :].rearrange("p c t -> p (c t)"),
            )

        def product(bank, lhs_codes, lhs_plane, t, rhs_codes, rhs_plane, cols):
            m = slice(t * P, (t + 1) * P)
            nc.tensor.matmul_mx(
                out=bank[:, cols],
                lhsT=lhs_codes[:, m].bitcast(FP8X4),
                lhsT_scale=lhs_plane[:, m],
                rhs=rhs_codes[:, cols].bitcast(FP8X4),
                rhs_scale=rhs_plane[:, cols],
                start=True,
                stop=True,
            )

        whole = slice(0, S)
        halves = [slice(0, HALF), slice(HALF, S)]

        def pieces(t):
            return halves if t == PACK - 1 else [whole]

        x_plane = sbuf("x_plane", [P, T], U8)
        w1_plane_raw = keep.tile([P, H], U8, name="w1_plane_raw", tag="w1_plane_then_cb_codes", align_bytes=64)
        nc.vector.memset(x_plane[:, :VECTOR_CLEARS].bitcast(I32), 0)
        nc.gpsimd.memset(x_plane[:, VECTOR_CLEARS:].bitcast(I32), 0)
        nc.gpsimd.memset(w1_plane_raw[:].bitcast(I32), 0)
        x_codes = sbuf("x_codes", [P, T], I32)
        w1_codes_raw = sbuf("w1_codes_raw", [P, H], I32)
        offs_list = load_list("offs_list", offs)
        cb_list = load_list("cb_list", cb)
        n1_list = load_list("n1_list", n1)
        load_plane(x_plane, x_scales)
        nc.sync.dma_start(x_codes[:], dram_words(x_words))
        load_plane(w1_plane_raw, w1_scales)
        nc.sync.dma_start(w1_codes_raw[:], dram_words(w1_words))
        n2_list = load_list("n2_list", n2)
        cand_list = load_list("cand_list", cand)
        gain = sbuf("gain", [P, PACK], F32)
        nc.sync.dma_start(gain[:], gs.rearrange("(p t) o -> p (t o)", t=PACK))
        wb_rows = sbuf("wb_rows", [P, PACK, S], F32)
        nc.sync.dma_start(wb_rows[:], wb.rearrange("(p t) n -> p t n", t=PACK))
        n4_list = load_list("n4_list", n4)
        n5_list = load_list("n5_list", n5)
        n3_list = load_list("n3_list", n3)
        z_factor = sbuf("z_factor", [P, PACK], F32)
        nc.gpsimd.tensor_scalar(z_factor[:], gain[:], 0.75, 0.0, ALU.mult, ALU.add)

        xq_codes = sbuf("xq_codes", [P, S], U32)
        xq_plane = sbuf("xq_plane", [P, S], U8)
        cb_codes = keep.tile([P, C], U32, name="cb_codes", tag="w1_plane_then_cb_codes", align_bytes=64)
        cb_plane = sbuf("cb_plane", [P, C], U8)
        cand_codes = sbuf("cand_codes", [P, C], U32)
        cand_plane = sbuf("cand_plane", [P, C], U8)
        w1_codes = sbuf("w1_codes", [P, H], U32)
        w1_plane = sbuf("w1_plane", [P, H], U8)
        x_window = x_codes[:].bitcast(U32)

        deal(nc.scalar.copy, w1_codes[:], w1_codes_raw[:].bitcast(U32))
        nc.vector.tensor_copy(xq_plane[:], x_plane[:].indirect(offs_list[:]))
        nc.vector.tensor_copy(xq_codes[:], x_window.indirect(offs_list[:]))
        deal(nc.vector.tensor_copy, w1_plane[:], w1_plane_raw[:])

        ya_window = [sbuf("ya_window%d" % t, [P, 2 * S], F32) for t in range(PACK)]
        b_window = [sbuf("b_window%d" % t, [P, 3 * S], F32) for t in range(PACK)]
        for t in range(PACK):
            nc.vector.memset(ya_window[t][:, S:].bitcast(I32), 0)
        y_banks = [psum.tile([P, S], F32, name="y_bank%d" % t, tag="y_then_a%d" % t) for t in range(PACK)]
        for t in range(PACK):
            product(y_banks[t], w1_codes, w1_plane, t, xq_codes, xq_plane, whole)
        nc.vector.tensor_copy(dealt(cb_plane), x_plane[:].indirect(cb_list[:]))
        nc.vector.tensor_copy(dealt(cb_codes), x_window.indirect(cb_list[:]))
        nc.vector.tensor_copy(dealt(cand_plane), x_plane[:].indirect(cand_list[:]))
        nc.vector.tensor_copy(dealt(cand_codes), x_window.indirect(cand_list[:]))

        wb_grouped = sbuf("wb_grouped", [P, S, PACK], BF16)
        wb_codes = sbuf("wb_codes", [P, S], U32)
        wb_plane = sbuf("wb_plane", [P, S], U8)
        for cols in halves:
            round_and_group(nc.vector.tensor_copy, wb_grouped, wb_rows, cols)
        quantize(wb_codes, wb_plane, wb_grouped, whole)
        b_banks = [psum.tile([P, S], F32, name="b_bank%d" % t, tag="b%d" % t) for t in range(PACK)]
        for t in range(PACK):
            product(b_banks[t], cb_codes, cb_plane, t, wb_codes, wb_plane, whole)

        y_diff = [b_window[t][:, S:].rearrange("p (side c) -> p side c", side=2) for t in range(PACK)]
        z_rows = sbuf("z_rows", [P, PACK, S], F32)

        def multiply_differences(t):
            for cols in pieces(t):
                nc.vector.scalar_tensor_tensor(
                    z_rows[:, t, cols],
                    y_diff[t][:, 0, cols],
                    z_factor[:, t : t + 1],
                    y_diff[t][:, 1, cols],
                    ALU.mult,
                    ALU.mult,
                )

        for t in range(PACK):
            y_rows = ya_window[t][:, :S]
            nc.scalar.copy(y_rows, y_banks[t][:])
            if t % 2 == 1:
                y_picked = sbuf("y_picked%d" % t, [P, 2, S], F32)
                for side, offsets in enumerate((n1_list, n2_list)):
                    nc.scalar.activation(y_picked[:, side, :], ya_window[t][:].indirect(offsets[:]), COPY)
                nc.vector.tensor_tensor(
                    y_diff[t], y_picked[:], y_rows.unsqueeze(1).to_broadcast([P, 2, S]), ALU.subtract
                )
            else:
                y_copy = sbuf("y_copy%d" % t, [P, S], F32)
                nc.scalar.copy(y_copy[:], y_banks[t][:])
                for side, offsets in enumerate((n1_list, n2_list)):
                    nc.vector.tensor_tensor(
                        y_diff[t][:, side, :], ya_window[t][:].indirect(offsets[:]), y_copy[:], ALU.subtract
                    )
            if t > 0:
                multiply_differences(t - 1)
        multiply_differences(PACK - 1)

        z_grouped = sbuf("z_grouped", [P, S, PACK], BF16)
        z_codes = sbuf("z_codes", [P, S], U32)
        z_plane = sbuf("z_plane", [P, S], U8)
        a_banks = [psum.tile([P, S], F32, name="a_bank%d" % t, tag="y_then_a%d" % t) for t in range(PACK)]
        for cols in halves:
            round_and_group(nc.vector.tensor_copy, z_grouped, z_rows, cols)
        for cols in halves:
            quantize(z_codes, z_plane, z_grouped, cols)
        for t in range(PACK):
            for cols in halves:
                product(a_banks[t], cand_codes, cand_plane, t, z_codes, z_plane, cols)

        result = sbuf("result", [P, PACK, S], F32)
        out_rows = out_0.rearrange("(p t) n -> p t n", t=PACK)
        for t in range(PACK):
            half_a = ya_window[t][:, :S]
            if t == 0:
                nc.vector.tensor_scalar(half_a, a_banks[t][:], 1.0 / 32, None, ALU.mult)
            else:
                nc.scalar.activation(half_a, a_banks[t][:], COPY, scale=1.0 / 32)
            nc.scalar.copy(b_window[t][:, :S], b_banks[t][:])
            upper = keep.tile([P, S], F32, name="upper", bufs=UPPER_BUFS)
            lower = keep.tile([P, S], F32, name="lower", bufs=LOWER_BUFS)
            half_a_picked = keep.tile([P, S], F32, name="half_a_picked", bufs=PACK)
            score = keep.tile([P, S], F32, name="score", bufs=PACK)
            capped = keep.tile([P, S], F32, name="capped", bufs=PACK)
            look_up(t == 0, half_a_picked[:], ya_window[t], n3_list)
            look_up(False, upper[:], b_window[t], n4_list)
            look_up(False, lower[:], b_window[t], n5_list)
            nc.vector.scalar_tensor_tensor(score[:], half_a, 2.0, half_a_picked[:], ALU.mult, ALU.subtract)
            nc.vector.tensor_tensor(capped[:], score[:], upper[:], ALU.min)
            for cols in pieces(t):
                nc.vector.tensor_tensor(result[:, t, cols], capped[:, cols], lower[:, cols], ALU.max)
            nc.sync.dma_start(out_rows[:, t, :], result[:, t, :])

        out_grouped = sbuf("out_grouped", [P, S, PACK], BF16)
        out_codes = sbuf("out_codes", [P, S], U32)
        out_plane = sbuf("out_plane", [P, S], U8)
        round_and_group(nc.scalar.copy, out_grouped, result, halves[0])
        round_and_group(nc.vector.tensor_copy, out_grouped, result, halves[1])
        for cols in reversed(halves):
            quantize(out_codes, out_plane, out_grouped, cols)
            nc.sync.dma_start(dram_words(out_1)[:, cols], out_codes[:, cols].bitcast(I32))
        for q in range(QUADRANTS):
            queue = nc.sync if q % 2 == 0 else nc.scalar
            queue.dma_start(dram_scale_rows(out_2, q), plane_rows(out_plane, q))
